import numpy as np
import ml_dtypes


def mxq(x, axis, fmt="e4m3"):
    dtype, down = {"e4m3": (ml_dtypes.float8_e4m3fn, 7), "e5m2": (ml_dtypes.float8_e5m2, 14)}[fmt]
    v = np.moveaxis(np.asarray(x, np.float32).astype(ml_dtypes.bfloat16).astype(np.float64), axis, -1)
    blocks = v.reshape(v.shape[:-1] + (-1, 32))
    amax = np.abs(blocks).max(-1, keepdims=True)
    byte = np.maximum(np.where(amax > 0, np.frexp(amax)[1] - 1 + 127, 0) - down, 1)
    scale = np.exp2(byte - 127.0)
    codes = (blocks / scale).astype(np.float32).astype(dtype).astype(np.float64)
    return np.moveaxis((codes * scale).reshape(v.shape), -1, axis)


WIDE = False


def mx_kscale(k):
    if not WIDE:
        return np.ones(k)
    levels = np.array([10, -10, 5, -5, 0])
    if k % 512:
        return np.exp2(np.random.permutation(np.resize(levels, k // 32))).repeat(32)
    a = np.empty((k // 512, 16))
    for p in range(k // 512):
        a[p, :8] = np.random.permutation(np.resize(levels, 8))
        for g in range(8):
            far = levels[np.abs(levels - a[p, g]) >= 10]
            a[p, g + 8] = far[np.random.randint(len(far))]
    return np.exp2(a.ravel()).repeat(32)


BF16 = ml_dtypes.bfloat16


def bf(x):
    return np.asarray(x, np.float32).astype(BF16)


def f64(x):
    return np.asarray(x).astype(np.float64)


E2M1 = np.array([0.0, 0.5, 1.0, 1.5, 2.0, 3.0, 4.0, 6.0, -0.0, -0.5, -1.0, -1.5, -2.0, -3.0, -4.0, -6.0])


def pack_weight(w, fmt):
    k, n = w.shape
    w = f64(bf(w)).reshape(k // 32, 32, n)
    amax = np.abs(w).max(1)
    if fmt == "e4m3":
        byte = np.frexp(amax)[1] - 1 + 127 - 7
    else:
        mant, ex = np.frexp(amax / 6.0)
        byte = np.where(mant > 0.5, ex, ex - 1) + 127
    byte = np.clip(np.where(amax > 0, byte, 1), 1, 254)
    scaled = (w * np.exp2(127.0 - byte)[:, None, :]).reshape(k, n).astype(np.float32)
    by_word = np.ascontiguousarray(scaled.reshape(k // 512, 128, 4, n).transpose(0, 1, 3, 2))
    if fmt == "e4m3":
        words = by_word.astype(ml_dtypes.float8_e4m3fn).view(np.uint8)
    else:
        c = by_word.astype(ml_dtypes.float4_e2m1fn).view(np.uint8) & 0xF
        words = c[..., 0::2] | (c[..., 1::2] << 4)
    return np.ascontiguousarray(words), np.ascontiguousarray(byte.astype(np.uint8).reshape(k // 512, 16, n))


def unpack_weight(words, scales, fmt):
    g, p, n, _ = words.shape
    if fmt == "e4m3":
        vals = np.ascontiguousarray(words).view(ml_dtypes.float8_e4m3fn).astype(np.float64)
    else:
        nib = np.empty((g, p, n, 4), np.uint8)
        nib[..., 0::2] = words & 0xF
        nib[..., 1::2] = words >> 4
        vals = E2M1[nib]
    vals = vals * np.repeat(np.exp2(scales.astype(np.float64) - 127.0), 8, axis=1)[..., None]
    return vals.transpose(0, 1, 3, 2).reshape(g * 512, n)
def pack4(w):
    words, scales = pack_weight(w, "e2m1")
    return words.reshape(words.shape[0], 128, -1), scales


def unpack4(words, scales):
    return unpack_weight(words.reshape(words.shape[0], 128, -1, 2), scales, "e2m1")


M, K, C, F, R = 1024, 1536, 1024, 2048, 512


def draw0():
    s = mx_kscale(K)
    t = mx_kscale(C)
    u = mx_kscale(M)
    x = np.random.standard_normal((M, K)) * s * u[:, None]
    w = np.random.standard_normal((K, C)) / np.sqrt(K) / s[:, None] * t
    prior = 0.5 * np.random.standard_normal((M, C)) * u[:, None] * t
    basis = 0.5 * np.random.standard_normal((C, F)) / np.sqrt(C) / t[:, None]
    depth = (1 + 0.1 * np.random.standard_normal(M)) / u
    pop = np.random.standard_normal((R, M)) / np.sqrt(M) / u
    basis_words, basis_scales = pack4(basis)
    return {"x": bf(x), "w": bf(w), "prior": bf(prior),
            "basis_words": basis_words, "basis_scales": basis_scales,
            "depth": bf(depth), "pop": bf(pop)}


def core(x, w, prior, basis_words, basis_scales, depth, pop):
    h = (mxq(f64(x), 1, "e4m3") @ mxq(f64(w), 0, "e4m3")) + f64(prior)
    logmag = mxq(h, 1, "e4m3") @ unpack4(basis_words, basis_scales)
    mag = np.exp(f64(depth)[:, None] * logmag)
    load = mxq(f64(pop), 1, "e4m3") @ mxq(h, 0, "e4m3")
    return mag, load


def e4m3fn_bytes(y):
    return np.clip(np.asarray(y, np.float64), -448.0, 448.0).astype(np.float32).astype(ml_dtypes.float8_e4m3fn).view(np.uint8)


def e4m3fn_values(b):
    return np.asarray(b, np.uint8).view(ml_dtypes.float8_e4m3fn).astype(np.float64)


def setup_inputs():
    d = draw0()
    x0 = np.asarray(d['pop']).astype(np.float64)
    s = (np.max(np.abs(x0), axis=(0,), keepdims=True) / 448.0).astype(np.float32)
    out = {}
    for k, v in d.items():
        if k == 'pop':
            out['pop_bytes'] = e4m3fn_bytes(x0 / s.astype(np.float64))
            out['pop_scale'] = s
        else:
            out[k] = v
    return out


def reference(x, w, prior, basis_words, basis_scales, depth, pop_bytes, pop_scale):
    return core(x, w, prior, basis_words, basis_scales, depth, e4m3fn_values(pop_bytes) * pop_scale.astype(np.float64))

@@ -1,0 +1,617 @@
+from contextlib import ExitStack
+
+import concourse.mybir as mybir
+from concourse.masks import make_identity
+
+M, K, C, F, R = 1024, 1536, 1024, 2048, 512
+FLOPS = 2 * (M * K * C + M * C * F + R * M * C)
+
+F32 = mybir.dt.float32
+BF16 = mybir.dt.bfloat16
+U32 = mybir.dt.uint32
+I32 = mybir.dt.int32
+U8 = mybir.dt.uint8
+E4M3 = mybir.dt.float8_e4m3fn_x4
+E2M1 = mybir.dt.float4_e2m1fn_x4
+FP8 = mybir.dt.float8_e4m3fn
+ADD = mybir.AluOpType.add
+MULT = mybir.AluOpType.mult
+EXP = mybir.ActivationFunctionType.Exp
+
+P = 128
+HALF = 512
+V_COLS = (288, 256)
+
+
+def tile_hrtf_weights_synthesis_s8_kernel(
+    tc, x, w, prior, basis_words, basis_scales, depth, pop_bytes, pop_scale, mag, load
+):
+    nc = tc.nc
+    with ExitStack() as ctx:
+        keep = ctx.enter_context(tc.tile_pool(name="keep", bufs=1))
+        stage = ctx.enter_context(tc.tile_pool(name="stage", bufs=4))
+        outs = ctx.enter_context(tc.tile_pool(name="outs", bufs=3))
+        psum = ctx.enter_context(tc.psum_pool(name="psum", bufs=8))
+        ctx.enter_context(tc.manual_schedule())
+
+        def bank():
+            b = psum.tile([P, 512], F32, name="bank")
+            return b
+
+        def kept(name, shape, dt):
+            t = keep.tile(shape, dt, name=name, align_bytes=64)
+            return t
+
+        ident = kept("ident", [P, P], F32)
+        dummy = kept("dummy", [P, 1], F32)
+        x_raw = [
+            outs.tile([P, 2, K], BF16, name="x_raw%d" % i, tag="big", bufs=4, align_bytes=64) for i in range(4)
+        ]
+        w_raw = [
+            [
+                outs.tile([P, 4, HALF], BF16, name="w_raw%d%d" % (h, q), tag="small", bufs=6, align_bytes=64)
+                for q in range(3)
+            ]
+            for h in range(2)
+        ]
+        pr = [[kept("pr%d%d" % (g, h), [P, 4, HALF], BF16) for h in range(2)] for g in range(2)]
+        b_words = kept("b_words", [P, 2, 2 * F], U8)
+        b_scales = kept("b_scales", [P, 2, F], U8)
+        depth_bf = kept("depth_bf", [P, 2, 4], BF16)
+        depth_f = kept("depth_f", [P, 8], F32)
+        pop_raw = kept("pop_raw", [P, 4, M], U8)
+        pop_sc = kept("pop_sc", [P, M], F32)
+        pop_bf = kept("pop_bf", [P, 4, M], BF16)
+        x_c = [kept("x_c%d" % i, [P, 3, 256], U32) for i in range(4)]
+        x_s = [kept("x_s%d" % i, [P, 3, 256], U8) for i in range(4)]
+        w_c = [[kept("w_c%d%d" % (h, q), [P, HALF], U32) for q in range(3)] for h in range(2)]
+        w_s = [[kept("w_s%d%d" % (h, q), [P, HALF], U8) for q in range(3)] for h in range(2)]
+        hb = [kept("hb%d" % g, [P, 4, C], BF16) for g in range(2)]
+        ht_c = [kept("ht_c%d" % i, [P, 2, P], U32) for i in range(8)]
+        ht_s = [kept("ht_s%d" % i, [P, 2, P], U8) for i in range(8)]
+        h_c = [kept("h_c%d" % g, [P, C], U32) for g in range(2)]
+        h_s = [kept("h_s%d" % g, [P, C], U8) for g in range(2)]
+        p_c = [kept("p_c%d" % g, [P, R], U32) for g in range(2)]
+        p_s = [kept("p_s%d" % g, [P, R], U8) for g in range(2)]
+
+        nc.vector.memset(dummy[:], 0.0)
+        nc.scalar.activation(out=dummy[:], in_=dummy[:], func=EXP)
+        make_identity(nc, ident[:])
+        nc.gpsimd.memset(b_scales[:].rearrange("p g n -> p (g n)").bitcast(I32), 0)
+
+        def load_x(i):
+            g, t0 = i // 2, 2 * (i % 2)
+            src = x[g * 512:(g + 1) * 512, :].rearrange("(p t) k -> p t k", t=4)
+            for a in range(2):
+                nc.sync.dma_start(out=x_raw[i][:, a, :], in_=src[:, t0 + a, :])
+
+        def load_w(h, q):
+            src = w[q * 512:(q + 1) * 512, h * HALF:(h + 1) * HALF]
+            nc.sync.dma_start(out=w_raw[h][q][:], in_=src.rearrange("(p j) c -> p j c", j=4))
+
+        def load_prior(g, h):
+            src = prior[g * 512:(g + 1) * 512, h * HALF:(h + 1) * HALF]
+            nc.sync.dma_start(out=pr[g][h][:], in_=src.rearrange("(p t) c -> p t c", t=4))
+
+        load_w(0, 1)
+        load_x(0)
+        load_w(0, 0)
+        load_x(1)
+        load_w(0, 2)
+        load_x(2)
+        load_w(1, 0)
+        load_w(1, 1)
+        load_x(3)
+        load_prior(0, 0)
+        load_w(1, 2)
+        load_prior(0, 1)
+        load_prior(1, 0)
+        nc.sync.dma_start(
+            out=b_words[:].rearrange("p g n -> p (g n)").bitcast(I32).rearrange("p (g n) -> p g n", g=2),
+            in_=basis_words.bitcast(I32).rearrange("g p n -> p g n"),
+        )
+        b_scales_i = b_scales[:].rearrange("p g n -> p (g n)").bitcast(I32).rearrange("p (g n) -> p g n", g=2)
+        for quad in range(4):
+            nc.sync.dma_start(
+                out=b_scales_i[32 * quad:32 * quad + 4],
+                in_=basis_scales.bitcast(I32)[:, 4 * quad:4 * quad + 4, :].rearrange("g r n -> r g n"),
+            )
+        nc.sync.dma_start(out=depth_bf[:], in_=depth.rearrange("(g p t) -> p g t", p=P, t=4))
+        nc.sync.dma_start(out=pop_raw[:], in_=pop_bytes.rearrange("(p a) k -> p a k", a=4))
+        nc.sync.dma_start(out=pop_sc[:], in_=pop_scale.rearrange("o k -> (o k)").partition_broadcast(P))
+        load_prior(1, 1)
+
+        def words(tile_ap):
+            return tile_ap.bitcast(F32)
+
+        x_banks = {}
+
+        def x_turn(i, a, q):
+            if (i, q) not in x_banks:
+                b = bank()
+                x_banks[i, q] = b
+            xw = words(x_raw[i][:, a, :])
+            for u in range(2):
+                col = (2 * a + u) * P
+                nc.tensor.transpose(x_banks[i, q][:, col:col + P], xw[:, 256 * q + u:256 * (q + 1):2], ident[:])
+
+        def copy(engine, out, in_):
+            if engine == "S":
+                nc.scalar.copy(out=out, in_=in_)
+            else:
+                nc.vector.tensor_copy(out=out, in_=in_)
+
+        x_grouped = {}
+
+        def x_empty(i, q, engine):
+            if i not in x_grouped:
+                xg = stage.tile([P, 3, 2, P, 4], BF16, name="xg", bufs=2, align_bytes=64)
+                x_grouped[i] = xg
+            copy(
+                engine,
+                words(x_grouped[i][:, q].rearrange("p a m t -> p (a m t)")).rearrange("p (a m u) -> p a m u", a=2, u=2),
+                x_banks[i, q][:].rearrange("p (a u m) -> p a m u", a=2, u=2),
+            )
+
+        def x_quant(i, q0, q1):
+            nc.vector.quantize_mx(
+                out=x_c[i][:, q0:q1, :].rearrange("p q m -> p (q m)").bitcast(E4M3),
+                scales=x_s[i][:, q0:q1, :].rearrange("p q m -> p (q m)"),
+                in_=x_grouped[i][:, q0:q1].rearrange("p q a m t -> p (q a m t)"),
+            )
+
+        w_grouped = {}
+
+        def w_group(h, q, engine):
+            if (h, q) not in w_grouped:
+                wg = stage.tile([P, HALF, 4], BF16, name="wg", bufs=3, align_bytes=64)
+                w_grouped[h, q] = wg
+            cols = slice(0, V_COLS[h]) if engine == "V" else slice(V_COLS[h], HALF)
+            copy(engine, w_grouped[h, q][:, cols, :], w_raw[h][q][:, :, cols].rearrange("p j c -> p c j"))
+
+        def w_quant(h, q):
+            nc.vector.quantize_mx(
+                out=w_c[h][q][:].bitcast(E4M3),
+                scales=w_s[h][q][:],
+                in_=w_grouped[h, q][:].rearrange("p c j -> p (c j)"),
+            )
+
+        h_banks = {}
+
+        def h_pass(i, h, q):
+            if q == 0:
+                b = bank()
+                h_banks[i, h] = b
+            cols = slice((i % 2) * P, (i % 2 + 1) * P)
+            nc.tensor.matmul_mx(
+                out=h_banks[i, h][:],
+                lhsT=x_c[i // 2][:, q, cols].bitcast(E4M3),
+                lhsT_scale=x_s[i // 2][:, q, cols],
+                rhs=w_c[h][q][:].bitcast(E4M3),
+                rhs_scale=w_s[h][q][:],
+                start=(q == 0),
+                stop=(q == 2),
+            )
+
+        def h_add(i, h):
+            g, t = i // 4, i % 4
+            nc.vector.tensor_tensor(
+                out=hb[g][:, t, h * HALF:(h + 1) * HALF].rearrange("q (u p e) -> q u p e", u=2, e=2),
+                in0=h_banks[i, h][:].rearrange("q (p u e) -> q u p e", u=2, e=2),
+                in1=pr[g][h][:, t, :].rearrange("q (p u e) -> q u p e", u=2, e=2),
+                op=ADD,
+            )
+
+        ht_banks = {}
+
+        def ht_turn(i):
+            g, t = i // 4, i % 4
+            b = bank()
+            ht_banks[i] = b
+            hw = words(hb[g][:, t, :])
+            for v in range(4):
+                nc.tensor.transpose(b[:, v * P:(v + 1) * P], hw[:, v * P:(v + 1) * P], ident[:])
+
+        ht_grouped = {}
+
+        def ht_empty(i, engine):
+            hg = stage.tile([P, 2, P, 4], BF16, name="hg", align_bytes=64)
+            ht_grouped[i] = hg
+            copy(
+                engine,
+                words(hg[:].rearrange("p a m t -> p (a m t)")).rearrange("p (a m u) -> p a m u", a=2, u=2),
+                ht_banks[i][:].rearrange("p (a u m) -> p a m u", a=2, u=2),
+            )
+
+        def ht_quant(i):
+            nc.vector.quantize_mx(
+                out=ht_c[i][:].rearrange("p a m -> p (a m)").bitcast(E4M3),
+                scales=ht_s[i][:].rearrange("p a m -> p (a m)"),
+                in_=ht_grouped[i][:].rearrange("p a m t -> p (a m t)"),
+            )
+
+        mag_rows = mag.rearrange("(g p t) f -> g t p f", p=P, t=4)
+        mag_banks = {}
+
+        def mag_mm(i, f):
+            b = bank()
+            mag_banks[i, f] = b
+            for a in range(2):
+                nc.tensor.matmul_mx(
+                    out=b[:],
+                    lhsT=ht_c[i][:, a, :].bitcast(E4M3),
+                    lhsT_scale=ht_s[i][:, a, :],
+                    rhs=b_words[:, a, 1024 * f:1024 * (f + 1)].bitcast(E2M1),
+                    rhs_scale=b_scales[:, a, 512 * f:512 * (f + 1)],
+                    start=(a == 0),
+                    stop=(a == 1),
+                )
+
+        mag_tiles = {}
+
+        def mag_exp(i, f):
+            if f == 0:
+                mo = outs.tile([P, F], F32, name="mo", tag="big", bufs=4, align_bytes=64)
+                mag_tiles[i] = mo
+            nc.scalar.activation(
+                out=mag_tiles[i][:, 512 * f:512 * (f + 1)], in_=mag_banks[i, f][:], func=EXP, scale=depth_f[:, i:i + 1]
+            )
+
+        def mag_store(i, z):
+            cols = slice(1024 * z, 1024 * (z + 1))
+            nc.sync.dma_start(out=mag_rows[i // 4, i % 4, :, cols], in_=mag_tiles[i][:, cols])
+
+        h_grouped = {}
+
+        def h_group(g, h, engine):
+            group = stage.tile([P, HALF, 4], BF16, name="group", bufs=3, align_bytes=64)
+            h_grouped[g, h] = group
+            cols = slice(HALF * h, HALF * (h + 1))
+            copy(engine, group[:], hb[g][:, :, cols].rearrange("p t c -> p c t"))
+
+        def h_quant(g, h):
+            cols = slice(HALF * h, HALF * (h + 1))
+            nc.vector.quantize_mx(
+                out=h_c[g][:, cols].bitcast(E4M3),
+                scales=h_s[g][:, cols],
+                in_=h_grouped[g, h][:].rearrange("p c t -> p (c t)"),
+            )
+
+        pop_banks = {}
+
+        def pop_product(a):
+            nc.vector.tensor_tensor(out=pop_bf[:, a, :], in0=pop_raw[:, a, :].bitcast(FP8), in1=pop_sc[:], op=MULT)
+
+        def pop_turn(g, z):
+            b = bank()
+            pop_banks[g, z] = b
+            for a in range(2):
+                pw = words(pop_bf[:, 2 * z + a, :])
+                for u in range(2):
+                    col = (2 * a + u) * P
+                    nc.tensor.transpose(b[:, col:col + P], pw[:, 256 * g + u:256 * (g + 1):2], ident[:])
+
+        pop_grouped = {}
+
+        def pop_empty(g, z, engine):
+            if g not in pop_grouped:
+                group = stage.tile([P, 2, 2, P, 4], BF16, name="group", bufs=3, align_bytes=64)
+                pop_grouped[g] = group
+            copy(
+                engine,
+                words(pop_grouped[g][:, z].rearrange("p a r t -> p (a r t)")).rearrange("p (a r u) -> p a r u", a=2, u=2),
+                pop_banks[g, z][:].rearrange("p (a u r) -> p a r u", a=2, u=2),
+            )
+
+        def pop_quant(g):
+            nc.vector.quantize_mx(
+                out=p_c[g][:].bitcast(E4M3),
+                scales=p_s[g][:],
+                in_=pop_grouped[g][:].rearrange("p z a r t -> p (z a r t)"),
+            )
+
+        load_rows = load.rearrange("(p a) c -> a p c", a=4)
+        load_banks = {}
+
+        def load_mm(a, h):
+            b = bank()
+            load_banks[a, h] = b
+            for g in range(2):
+                nc.tensor.matmul_mx(
+                    out=b[:],
+                    lhsT=p_c[g][:, P * a:P * (a + 1)].bitcast(E4M3),
+                    lhsT_scale=p_s[g][:, P * a:P * (a + 1)],
+                    rhs=h_c[g][:, 512 * h:512 * (h + 1)].bitcast(E4M3),
+                    rhs_scale=h_s[g][:, 512 * h:512 * (h + 1)],
+                    start=(g == 0),
+                    stop=(g == 1),
+                )
+
+        load_tiles = {}
+
+        def load_empty(a, h, engine):
+            if a not in load_tiles:
+                lo = outs.tile([P, C], F32, name="lo", tag="small", bufs=6, align_bytes=64)
+                load_tiles[a] = lo
+            copy(
+                engine,
+                load_tiles[a][:, 512 * h:512 * (h + 1)].rearrange("q (p u e) -> q p u e", u=2, e=2),
+                load_banks[a, h][:].rearrange("q (u p e) -> q p u e", u=2, e=2),
+            )
+
+        def load_store(a):
+            nc.sync.dma_start(out=load_rows[a], in_=load_tiles[a][:])
+
+        w_group(0, 1, "V")
+        w_group(0, 1, "S")
+        x_turn(0, 0, 0)
+        x_turn(0, 0, 1)
+        w_quant(0, 1)
+        x_turn(0, 0, 2)
+        x_turn(0, 1, 0)
+        x_turn(0, 1, 1)
+        x_empty(0, 0, "V")
+        x_turn(0, 1, 2)
+        x_empty(0, 1, "S")
+        x_empty(0, 2, "V")
+        w_group(0, 0, "S")
+        w_group(0, 0, "V")
+        x_turn(1, 0, 0)
+        x_quant(0, 0, 2)
+        x_turn(1, 0, 1)
+        x_turn(1, 0, 2)
+        w_quant(0, 0)
+        x_turn(1, 1, 0)
+        x_turn(1, 1, 1)
+        x_empty(1, 0, "S")
+        x_quant(0, 2, 3)
+        x_turn(1, 1, 2)
+        h_pass(0, 0, 0)
+        x_empty(1, 1, "V")
+        x_empty(1, 2, "S")
+        h_pass(1, 0, 0)
+        h_pass(0, 0, 1)
+        w_group(0, 2, "V")
+        w_group(0, 2, "S")
+        h_pass(1, 0, 1)
+        x_turn(2, 0, 0)
+        x_quant(1, 0, 2)
+        x_turn(2, 0, 1)
+        x_turn(2, 0, 2)
+        w_quant(0, 2)
+        h_pass(2, 0, 0)
+        x_turn(2, 1, 0)
+        x_quant(1, 2, 3)
+        x_turn(2, 1, 1)
+        x_empty(2, 0, "S")
+        x_turn(2, 1, 2)
+        x_empty(2, 1, "V")
+        h_pass(0, 0, 2)
+        x_empty(2, 2, "S")
+        h_pass(1, 0, 2)
+        w_group(1, 0, "V")
+        h_pass(2, 0, 1)
+        w_group(1, 0, "S")
+        h_pass(3, 0, 0)
+        h_pass(2, 0, 2)
+        x_quant(2, 0, 2)
+        h_pass(3, 0, 1)
+        h_pass(3, 0, 2)
+        w_group(1, 1, "V")
+        w_group(1, 1, "S")
+        h_pass(4, 0, 0)
+        h_pass(5, 0, 0)
+        w_quant(1, 0)
+        x_turn(3, 0, 0)
+        x_turn(3, 0, 1)
+        h_pass(4, 0, 1)
+        x_quant(2, 2, 3)
+        h_pass(5, 0, 1)
+        w_quant(1, 1)
+        x_turn(3, 1, 0)
+        x_turn(3, 1, 1)
+        x_empty(3, 0, "S")
+        h_pass(4, 0, 2)
+        x_empty(3, 1, "V")
+        h_pass(5, 0, 2)
+        h_pass(0, 1, 0)
+        h_add(0, 0)
+        x_turn(3, 0, 2)
+        h_pass(0, 1, 1)
+        h_add(1, 0)
+        x_turn(3, 1, 2)
+        h_pass(1, 1, 0)
+        x_empty(3, 2, "S")
+        w_group(1, 2, "V")
+        h_pass(4, 1, 0)
+        h_pass(1, 1, 1)
+        w_group(1, 2, "S")
+        h_pass(2, 1, 0)
+        h_add(2, 0)
+        h_pass(4, 1, 1)
+        h_pass(2, 1, 1)
+        h_add(3, 0)
+        h_pass(3, 1, 0)
+        h_pass(3, 1, 1)
+        w_quant(1, 2)
+        h_group(0, 0, "S")
+        h_pass(5, 1, 0)
+        h_add(4, 0)
+        h_pass(5, 1, 1)
+        h_pass(0, 1, 2)
+        h_pass(1, 1, 2)
+        x_quant(3, 0, 2)
+        h_pass(2, 1, 2)
+        h_pass(4, 1, 2)
+        h_add(0, 1)
+        h_pass(3, 1, 2)
+        h_pass(7, 0, 0)
+        h_add(1, 1)
+        h_pass(5, 1, 2)
+        ht_turn(0)
+        h_add(2, 1)
+        ht_turn(1)
+        ht_empty(0, "S")
+        h_add(3, 1)
+        h_pass(7, 0, 1)
+        ht_empty(1, "S")
+        ht_turn(2)
+        nc.vector.tensor_copy(out=depth_f[:], in_=depth_bf[:].rearrange("p g t -> p (g t)"))
+        ht_quant(0)
+        ht_turn(3)
+        ht_empty(2, "S")
+        x_quant(3, 2, 3)
+        mag_mm(0, 0)
+        ht_quant(1)
+        ht_empty(3, "S")
+        ht_quant(2)
+        mag_mm(0, 1)
+        h_add(5, 0)
+        mag_exp(0, 0)
+        mag_mm(0, 2)
+        ht_quant(3)
+        mag_exp(0, 1)
+        mag_mm(0, 3)
+        h_group(0, 1, "V")
+        mag_exp(0, 2)
+        mag_mm(1, 0)
+        mag_store(0, 0)
+        mag_exp(0, 3)
+        mag_mm(1, 1)
+        h_add(4, 1)
+        mag_mm(1, 2)
+        mag_exp(1, 0)
+        mag_store(0, 1)
+        h_add(5, 1)
+        mag_mm(1, 3)
+        mag_exp(1, 1)
+        h_quant(0, 0)
+        mag_mm(2, 0)
+        mag_exp(1, 2)
+        mag_store(1, 0)
+        mag_mm(2, 1)
+        h_quant(0, 1)
+        mag_exp(1, 3)
+        mag_mm(2, 2)
+        pop_product(0)
+        mag_exp(2, 0)
+        mag_store(1, 1)
+        mag_mm(2, 3)
+        mag_exp(2, 1)
+        mag_mm(3, 0)
+        pop_product(1)
+        mag_exp(2, 2)
+        mag_store(2, 0)
+        mag_mm(3, 1)
+        mag_exp(2, 3)
+        mag_mm(3, 2)
+        pop_product(2)
+        mag_exp(3, 0)
+        h_pass(7, 1, 0)
+        mag_store(2, 1)
+        h_pass(7, 0, 2)
+        h_pass(7, 1, 1)
+        mag_exp(3, 1)
+        h_add(7, 0)
+        mag_mm(3, 3)
+        mag_exp(3, 2)
+        mag_store(3, 0)
+        h_pass(7, 1, 2)
+        pop_product(3)
+        h_pass(6, 0, 0)
+        mag_exp(3, 3)
+        ht_turn(4)
+        h_pass(6, 0, 1)
+        ht_empty(4, "S")
+        h_add(7, 1)
+        mag_store(3, 1)
+        h_pass(6, 1, 0)
+        h_pass(6, 0, 2)
+        h_pass(6, 1, 1)
+        ht_quant(4)
+        ht_turn(5)
+        h_add(6, 0)
+        mag_mm(4, 0)
+        ht_empty(5, "S")
+        h_group(1, 0, "V")
+        mag_mm(4, 1)
+        mag_exp(4, 0)
+        mag_mm(4, 2)
+        mag_exp(4, 1)
+        mag_mm(4, 3)
+        ht_quant(5)
+        mag_exp(4, 2)
+        mag_store(4, 0)
+        h_quant(1, 0)
+        h_pass(6, 1, 2)
+        mag_mm(5, 0)
+        mag_exp(4, 3)
+        h_add(6, 1)
+        mag_mm(5, 1)
+        mag_exp(5, 0)
+        mag_store(4, 1)
+        h_group(1, 1, "V")
+        mag_mm(5, 2)
+        mag_exp(5, 1)
+        mag_mm(5, 3)
+        mag_exp(5, 2)
+        mag_store(5, 0)
+        ht_turn(6)
+        mag_exp(5, 3)
+        h_quant(1, 1)
+        ht_turn(7)
+        pop_turn(0, 0)
+        ht_empty(6, "S")
+        ht_empty(7, "V")
+        mag_store(5, 1)
+        pop_turn(1, 0)
+        pop_empty(0, 0, "S")
+        ht_quant(6)
+        pop_turn(0, 1)
+        ht_quant(7)
+        pop_empty(1, 0, "S")
+        mag_mm(6, 0)
+        pop_empty(0, 1, "V")
+        mag_mm(6, 1)
+        mag_exp(6, 0)
+        pop_quant(0)
+        mag_mm(6, 2)
+        mag_exp(6, 1)
+        mag_mm(6, 3)
+        mag_exp(6, 2)
+        mag_store(6, 0)
+        mag_mm(7, 0)
+        mag_exp(6, 3)
+        pop_turn(1, 1)
+        mag_exp(7, 0)
+        mag_store(6, 1)
+        mag_mm(7, 1)
+        pop_empty(1, 1, "V")
+        mag_mm(7, 2)
+        mag_exp(7, 1)
+        pop_quant(1)
+        mag_mm(7, 3)
+        mag_exp(7, 2)
+        mag_store(7, 0)
+        load_mm(0, 0)
+        mag_exp(7, 3)
+        load_mm(0, 1)
+        load_empty(0, 0, "V")
+        mag_store(7, 1)
+        load_mm(1, 0)
+        load_empty(0, 1, "S")
+        load_mm(1, 1)
+        load_empty(1, 0, "V")
+        load_store(0)
+        load_mm(2, 0)
+        load_empty(1, 1, "S")
+        load_mm(2, 1)
+        load_empty(2, 0, "V")
+        load_store(1)
+        load_mm(3, 0)
+        load_empty(2, 1, "S")
+        load_mm(3, 1)
+        load_empty(3, 0, "V")
+        load_store(2)
+        load_empty(3, 1, "S")
+        load_store(3)

@@ -20,7 +20,7 @@ EXP = mybir.ActivationFunctionType.Exp
 
 P = 128
 HALF = 512
-V_COLS = (288, 256)
+V_COLS = (224, 208)
 
 
 def tile_hrtf_weights_synthesis_s8_kernel(
@@ -44,6 +44,7 @@ def tile_hrtf_weights_synthesis_s8_kernel(
 
         ident = kept("ident", [P, P], F32)
         dummy = kept("dummy", [P, 1], F32)
+        zeros = kept("zeros", [P, 512], BF16)
         x_raw = [
             outs.tile([P, 2, K], BF16, name="x_raw%d" % i, tag="big", bufs=4, align_bytes=64) for i in range(4)
         ]
@@ -54,7 +55,7 @@ def tile_hrtf_weights_synthesis_s8_kernel(
             ]
             for h in range(2)
         ]
-        pr = [[kept("pr%d%d" % (g, h), [P, 4, HALF], BF16) for h in range(2)] for g in range(2)]
+        pr = [[kept("pr%d%d" % (g, z), [P, 2, C], BF16) for z in range(2)] for g in range(2)]
         b_words = kept("b_words", [P, 2, 2 * F], U8)
         b_scales = kept("b_scales", [P, 2, F], U8)
         depth_bf = kept("depth_bf", [P, 2, 4], BF16)
@@ -74,6 +75,7 @@ def tile_hrtf_weights_synthesis_s8_kernel(
         p_c = [kept("p_c%d" % g, [P, R], U32) for g in range(2)]
         p_s = [kept("p_s%d" % g, [P, R], U8) for g in range(2)]
 
+        nc.vector.memset(zeros[:], 0.0)
         nc.vector.memset(dummy[:], 0.0)
         nc.scalar.activation(out=dummy[:], in_=dummy[:], func=EXP)
         make_identity(nc, ident[:])
@@ -89,23 +91,23 @@ def tile_hrtf_weights_synthesis_s8_kernel(
             src = w[q * 512:(q + 1) * 512, h * HALF:(h + 1) * HALF]
             nc.sync.dma_start(out=w_raw[h][q][:], in_=src.rearrange("(p j) c -> p j c", j=4))
 
-        def load_prior(g, h):
-            src = prior[g * 512:(g + 1) * 512, h * HALF:(h + 1) * HALF]
-            nc.sync.dma_start(out=pr[g][h][:], in_=src.rearrange("(p t) c -> p t c", t=4))
+        def load_prior(g, z):
+            src = prior[g * 512:(g + 1) * 512, :].rearrange("(p t) c -> p t c", t=4)
+            nc.sync.dma_start(out=pr[g][z][:], in_=src[:, 2 * z:2 * z + 2, :])
 
-        load_w(0, 1)
-        load_x(0)
         load_w(0, 0)
+        load_x(0)
+        load_w(0, 1)
         load_x(1)
-        load_w(0, 2)
         load_x(2)
+        load_w(0, 2)
         load_w(1, 0)
-        load_w(1, 1)
         load_x(3)
-        load_prior(0, 0)
+        load_w(1, 1)
         load_w(1, 2)
-        load_prior(0, 1)
-        load_prior(1, 0)
+        for g in range(2):
+            for z in range(2):
+                load_prior(g, z)
         nc.sync.dma_start(
             out=b_words[:].rearrange("p g n -> p (g n)").bitcast(I32).rearrange("p (g n) -> p g n", g=2),
             in_=basis_words.bitcast(I32).rearrange("g p n -> p g n"),
@@ -119,21 +121,29 @@ def tile_hrtf_weights_synthesis_s8_kernel(
         nc.sync.dma_start(out=depth_bf[:], in_=depth.rearrange("(g p t) -> p g t", p=P, t=4))
         nc.sync.dma_start(out=pop_raw[:], in_=pop_bytes.rearrange("(p a) k -> p a k", a=4))
         nc.sync.dma_start(out=pop_sc[:], in_=pop_scale.rearrange("o k -> (o k)").partition_broadcast(P))
-        load_prior(1, 1)
 
         def words(tile_ap):
             return tile_ap.bitcast(F32)
 
         x_banks = {}
 
-        def x_turn(i, a, q):
-            if (i, q) not in x_banks:
+        def x_turn(i):
+            for q in range(3):
                 b = bank()
                 x_banks[i, q] = b
-            xw = words(x_raw[i][:, a, :])
-            for u in range(2):
-                col = (2 * a + u) * P
-                nc.tensor.transpose(x_banks[i, q][:, col:col + P], xw[:, 256 * q + u:256 * (q + 1):2], ident[:])
+            for a in range(2):
+                xw = words(x_raw[i][:, a, :])
+                for q in range(3):
+                    for u in range(2):
+                        col = (2 * a + u) * P
+                        nc.tensor.transpose(
+                            x_banks[i, q][:, col:col + P], xw[:, 256 * q + u:256 * (q + 1):2], ident[:]
+                        )
+
+        def warm(n):
+            b = bank()
+            for k in range(n):
+                nc.tensor.matmul(b[:], lhsT=zeros[:, 0:P], rhs=zeros[:], start=True, stop=True)
 
         def copy(engine, out, in_):
             if engine == "S":
@@ -153,12 +163,13 @@ def tile_hrtf_weights_synthesis_s8_kernel(
                 x_banks[i, q][:].rearrange("p (a u m) -> p a m u", a=2, u=2),
             )
 
-        def x_quant(i, q0, q1):
-            nc.vector.quantize_mx(
-                out=x_c[i][:, q0:q1, :].rearrange("p q m -> p (q m)").bitcast(E4M3),
-                scales=x_s[i][:, q0:q1, :].rearrange("p q m -> p (q m)"),
-                in_=x_grouped[i][:, q0:q1].rearrange("p q a m t -> p (q a m t)"),
-            )
+        def x_quant(i):
+            for q0, q1 in ((0, 2), (2, 3)):
+                nc.vector.quantize_mx(
+                    out=x_c[i][:, q0:q1, :].rearrange("p q m -> p (q m)").bitcast(E4M3),
+                    scales=x_s[i][:, q0:q1, :].rearrange("p q m -> p (q m)"),
+                    in_=x_grouped[i][:, q0:q1].rearrange("p q a m t -> p (q a m t)"),
+                )
 
         w_grouped = {}
 
@@ -198,7 +209,7 @@ def tile_hrtf_weights_synthesis_s8_kernel(
             nc.vector.tensor_tensor(
                 out=hb[g][:, t, h * HALF:(h + 1) * HALF].rearrange("q (u p e) -> q u p e", u=2, e=2),
                 in0=h_banks[i, h][:].rearrange("q (p u e) -> q u p e", u=2, e=2),
-                in1=pr[g][h][:, t, :].rearrange("q (p u e) -> q u p e", u=2, e=2),
+                in1=pr[g][t // 2][:, t % 2, h * HALF:(h + 1) * HALF].rearrange("q (p u e) -> q u p e", u=2, e=2),
                 op=ADD,
             )
 
@@ -339,279 +350,136 @@ def tile_hrtf_weights_synthesis_s8_kernel(
                 load_banks[a, h][:].rearrange("q (u p e) -> q p u e", u=2, e=2),
             )
 
-        def load_store(a):
-            nc.sync.dma_start(out=load_rows[a], in_=load_tiles[a][:])
+        def load_store(a, halves):
+            for h in range(halves):
+                cols = slice(C // halves * h, C // halves * (h + 1))
+                nc.sync.dma_start(out=load_rows[a, :, cols], in_=load_tiles[a][:, cols])
 
-        w_group(0, 1, "V")
-        w_group(0, 1, "S")
-        x_turn(0, 0, 0)
-        x_turn(0, 0, 1)
-        w_quant(0, 1)
-        x_turn(0, 0, 2)
-        x_turn(0, 1, 0)
-        x_turn(0, 1, 1)
-        x_empty(0, 0, "V")
-        x_turn(0, 1, 2)
-        x_empty(0, 1, "S")
-        x_empty(0, 2, "V")
-        w_group(0, 0, "S")
-        w_group(0, 0, "V")
-        x_turn(1, 0, 0)
-        x_quant(0, 0, 2)
-        x_turn(1, 0, 1)
-        x_turn(1, 0, 2)
+
+        def x_step(i, vector_banks):
+            for q in range(3):
+                x_empty(i, q, "V" if q in vector_banks else "S")
+
+        def w_step(h, q):
+            w_group(h, q, "V")
+            w_group(h, q, "S")
+
+        def h_all(i, h):
+            for q in range(3):
+                h_pass(i, h, q)
+
+        def mag_step(i):
+            for f in range(4):
+                mag_mm(i, f)
+                mag_exp(i, f)
+                if f % 2:
+                    mag_store(i, f // 2)
+
+        def load_step(a, engines, halves=1):
+            for h in range(2):
+                load_mm(a, h)
+                load_empty(a, h, engines[h])
+            load_store(a, halves)
+
+        warm(8)
+        w_step(0, 0)
+        x_turn(0)
+        x_step(0, (1,))
         w_quant(0, 0)
-        x_turn(1, 1, 0)
-        x_turn(1, 1, 1)
-        x_empty(1, 0, "S")
-        x_quant(0, 2, 3)
-        x_turn(1, 1, 2)
-        h_pass(0, 0, 0)
-        x_empty(1, 1, "V")
-        x_empty(1, 2, "S")
-        h_pass(1, 0, 0)
-        h_pass(0, 0, 1)
-        w_group(0, 2, "V")
-        w_group(0, 2, "S")
-        h_pass(1, 0, 1)
-        x_turn(2, 0, 0)
-        x_quant(1, 0, 2)
-        x_turn(2, 0, 1)
-        x_turn(2, 0, 2)
+        w_step(0, 1)
+        x_quant(0)
+        warm(2)
+        x_turn(1)
+        x_step(1, (1,))
+        w_quant(0, 1)
+        x_quant(1)
+        x_turn(2)
+        w_step(0, 2)
+        x_step(2, (0, 1))
         w_quant(0, 2)
-        h_pass(2, 0, 0)
-        x_turn(2, 1, 0)
-        x_quant(1, 2, 3)
-        x_turn(2, 1, 1)
-        x_empty(2, 0, "S")
-        x_turn(2, 1, 2)
-        x_empty(2, 1, "V")
-        h_pass(0, 0, 2)
-        x_empty(2, 2, "S")
-        h_pass(1, 0, 2)
-        w_group(1, 0, "V")
-        h_pass(2, 0, 1)
-        w_group(1, 0, "S")
-        h_pass(3, 0, 0)
-        h_pass(2, 0, 2)
-        x_quant(2, 0, 2)
-        h_pass(3, 0, 1)
-        h_pass(3, 0, 2)
-        w_group(1, 1, "V")
-        w_group(1, 1, "S")
-        h_pass(4, 0, 0)
-        h_pass(5, 0, 0)
+        x_quant(2)
+        for q in range(2):
+            for i in range(4):
+                h_pass(i, 0, q)
+        x_turn(3)
+        w_step(1, 0)
+        x_step(3, (1,))
         w_quant(1, 0)
-        x_turn(3, 0, 0)
-        x_turn(3, 0, 1)
-        h_pass(4, 0, 1)
-        x_quant(2, 2, 3)
-        h_pass(5, 0, 1)
+        x_quant(3)
+        for i in range(4):
+            h_pass(i, 0, 2)
+        h_all(4, 0)
+        h_all(5, 0)
+        w_step(1, 1)
+        w_step(1, 2)
         w_quant(1, 1)
-        x_turn(3, 1, 0)
-        x_turn(3, 1, 1)
-        x_empty(3, 0, "S")
-        h_pass(4, 0, 2)
-        x_empty(3, 1, "V")
-        h_pass(5, 0, 2)
-        h_pass(0, 1, 0)
         h_add(0, 0)
-        x_turn(3, 0, 2)
-        h_pass(0, 1, 1)
-        h_add(1, 0)
-        x_turn(3, 1, 2)
-        h_pass(1, 1, 0)
-        x_empty(3, 2, "S")
-        w_group(1, 2, "V")
-        h_pass(4, 1, 0)
-        h_pass(1, 1, 1)
-        w_group(1, 2, "S")
-        h_pass(2, 1, 0)
-        h_add(2, 0)
-        h_pass(4, 1, 1)
-        h_pass(2, 1, 1)
-        h_add(3, 0)
-        h_pass(3, 1, 0)
-        h_pass(3, 1, 1)
         w_quant(1, 2)
-        h_group(0, 0, "S")
-        h_pass(5, 1, 0)
-        h_add(4, 0)
-        h_pass(5, 1, 1)
-        h_pass(0, 1, 2)
-        h_pass(1, 1, 2)
-        x_quant(3, 0, 2)
-        h_pass(2, 1, 2)
-        h_pass(4, 1, 2)
-        h_add(0, 1)
-        h_pass(3, 1, 2)
-        h_pass(7, 0, 0)
-        h_add(1, 1)
-        h_pass(5, 1, 2)
-        ht_turn(0)
-        h_add(2, 1)
-        ht_turn(1)
-        ht_empty(0, "S")
-        h_add(3, 1)
-        h_pass(7, 0, 1)
-        ht_empty(1, "S")
-        ht_turn(2)
-        nc.vector.tensor_copy(out=depth_f[:], in_=depth_bf[:].rearrange("p g t -> p (g t)"))
-        ht_quant(0)
-        ht_turn(3)
-        ht_empty(2, "S")
-        x_quant(3, 2, 3)
-        mag_mm(0, 0)
-        ht_quant(1)
-        ht_empty(3, "S")
-        ht_quant(2)
-        mag_mm(0, 1)
-        h_add(5, 0)
-        mag_exp(0, 0)
-        mag_mm(0, 2)
-        ht_quant(3)
-        mag_exp(0, 1)
-        mag_mm(0, 3)
-        h_group(0, 1, "V")
-        mag_exp(0, 2)
-        mag_mm(1, 0)
-        mag_store(0, 0)
-        mag_exp(0, 3)
-        mag_mm(1, 1)
-        h_add(4, 1)
-        mag_mm(1, 2)
-        mag_exp(1, 0)
-        mag_store(0, 1)
-        h_add(5, 1)
-        mag_mm(1, 3)
-        mag_exp(1, 1)
-        h_quant(0, 0)
-        mag_mm(2, 0)
-        mag_exp(1, 2)
-        mag_store(1, 0)
-        mag_mm(2, 1)
-        h_quant(0, 1)
-        mag_exp(1, 3)
-        mag_mm(2, 2)
-        pop_product(0)
-        mag_exp(2, 0)
-        mag_store(1, 1)
-        mag_mm(2, 3)
-        mag_exp(2, 1)
-        mag_mm(3, 0)
-        pop_product(1)
-        mag_exp(2, 2)
-        mag_store(2, 0)
-        mag_mm(3, 1)
-        mag_exp(2, 3)
-        mag_mm(3, 2)
-        pop_product(2)
-        mag_exp(3, 0)
-        h_pass(7, 1, 0)
-        mag_store(2, 1)
-        h_pass(7, 0, 2)
-        h_pass(7, 1, 1)
-        mag_exp(3, 1)
-        h_add(7, 0)
-        mag_mm(3, 3)
-        mag_exp(3, 2)
-        mag_store(3, 0)
-        h_pass(7, 1, 2)
-        pop_product(3)
-        h_pass(6, 0, 0)
-        mag_exp(3, 3)
-        ht_turn(4)
-        h_pass(6, 0, 1)
-        ht_empty(4, "S")
-        h_add(7, 1)
-        mag_store(3, 1)
-        h_pass(6, 1, 0)
-        h_pass(6, 0, 2)
-        h_pass(6, 1, 1)
-        ht_quant(4)
-        ht_turn(5)
+        for i in range(1, 6):
+            if i == 4:
+                h_all(0, 1)
+                h_all(1, 1)
+            h_add(i, 0)
+        h_all(2, 1)
+        h_all(3, 1)
+        for i in range(4):
+            h_add(i, 1)
+        h_all(6, 0)
+        h_all(7, 0)
+        for i in range(4):
+            ht_turn(i)
+        for i in range(4):
+            ht_empty(i, "SSSV"[i])
         h_add(6, 0)
-        mag_mm(4, 0)
+        ht_quant(0)
+        ht_quant(1)
+        h_add(7, 0)
+        ht_quant(2)
+        ht_quant(3)
+        nc.vector.tensor_copy(out=depth_f[:], in_=depth_bf[:].rearrange("p g t -> p (g t)"))
+        h_group(0, 0, "S")
+        for i in range(4, 8):
+            h_all(i, 1)
+        for i in range(4, 8):
+            h_add(i, 1)
+        mag_step(0)
+        mag_step(1)
+        h_group(0, 1, "V")
+        pop_product(0)
+        h_quant(0, 1)
+        for i in range(4, 8):
+            ht_turn(i)
+        ht_empty(4, "V")
         ht_empty(5, "S")
-        h_group(1, 0, "V")
-        mag_mm(4, 1)
-        mag_exp(4, 0)
-        mag_mm(4, 2)
-        mag_exp(4, 1)
-        mag_mm(4, 3)
+        pop_product(1)
+        ht_empty(6, "V")
+        ht_empty(7, "S")
+        ht_quant(4)
         ht_quant(5)
-        mag_exp(4, 2)
-        mag_store(4, 0)
-        h_quant(1, 0)
-        h_pass(6, 1, 2)
-        mag_mm(5, 0)
-        mag_exp(4, 3)
-        h_add(6, 1)
-        mag_mm(5, 1)
-        mag_exp(5, 0)
-        mag_store(4, 1)
-        h_group(1, 1, "V")
-        mag_mm(5, 2)
-        mag_exp(5, 1)
-        mag_mm(5, 3)
-        mag_exp(5, 2)
-        mag_store(5, 0)
-        ht_turn(6)
-        mag_exp(5, 3)
-        h_quant(1, 1)
-        ht_turn(7)
-        pop_turn(0, 0)
-        ht_empty(6, "S")
-        ht_empty(7, "V")
-        mag_store(5, 1)
-        pop_turn(1, 0)
-        pop_empty(0, 0, "S")
+        pop_product(2)
+        mag_step(2)
+        pop_product(3)
         ht_quant(6)
-        pop_turn(0, 1)
         ht_quant(7)
-        pop_empty(1, 0, "S")
-        mag_mm(6, 0)
-        pop_empty(0, 1, "V")
-        mag_mm(6, 1)
-        mag_exp(6, 0)
+        mag_step(3)
+        h_quant(0, 0)
+        mag_step(4)
+        for z in range(2):
+            for g in range(2):
+                pop_turn(g, z)
+        for z in range(2):
+            for g in range(2):
+                pop_empty(g, z, "VS"[z])
+        h_group(1, 0, "V")
         pop_quant(0)
-        mag_mm(6, 2)
-        mag_exp(6, 1)
-        mag_mm(6, 3)
-        mag_exp(6, 2)
-        mag_store(6, 0)
-        mag_mm(7, 0)
-        mag_exp(6, 3)
-        pop_turn(1, 1)
-        mag_exp(7, 0)
-        mag_store(6, 1)
-        mag_mm(7, 1)
-        pop_empty(1, 1, "V")
-        mag_mm(7, 2)
-        mag_exp(7, 1)
         pop_quant(1)
-        mag_mm(7, 3)
-        mag_exp(7, 2)
-        mag_store(7, 0)
-        load_mm(0, 0)
-        mag_exp(7, 3)
-        load_mm(0, 1)
-        load_empty(0, 0, "V")
-        mag_store(7, 1)
-        load_mm(1, 0)
-        load_empty(0, 1, "S")
-        load_mm(1, 1)
-        load_empty(1, 0, "V")
-        load_store(0)
-        load_mm(2, 0)
-        load_empty(1, 1, "S")
-        load_mm(2, 1)
-        load_empty(2, 0, "V")
-        load_store(1)
-        load_mm(3, 0)
-        load_empty(2, 1, "S")
-        load_mm(3, 1)
-        load_empty(3, 0, "V")
-        load_store(2)
-        load_empty(3, 1, "S")
-        load_store(3)
+        h_quant(1, 0)
+        h_group(1, 1, "V")
+        h_quant(1, 1)
+        mag_step(5)
+        mag_step(6)
+        load_step(0, "VV")
+        load_step(1, "VS")
+        load_step(2, "VV")
+        mag_step(7)
+        load_step(3, "VS", halves=2)

@@ -20,7 +20,7 @@ EXP = mybir.ActivationFunctionType.Exp
 
 P = 128
 HALF = 512
-V_COLS = (224, 208)
+V_COLS = (256, 224)
 
 
 def tile_hrtf_weights_synthesis_s8_kernel(
@@ -95,19 +95,20 @@ def tile_hrtf_weights_synthesis_s8_kernel(
             src = prior[g * 512:(g + 1) * 512, :].rearrange("(p t) c -> p t c", t=4)
             nc.sync.dma_start(out=pr[g][z][:], in_=src[:, 2 * z:2 * z + 2, :])
 
-        load_w(0, 0)
         load_x(0)
+        load_w(0, 0)
         load_w(0, 1)
         load_x(1)
         load_x(2)
         load_w(0, 2)
-        load_w(1, 0)
         load_x(3)
+        load_w(1, 0)
         load_w(1, 1)
+        load_prior(0, 0)
+        load_prior(0, 1)
         load_w(1, 2)
-        for g in range(2):
-            for z in range(2):
-                load_prior(g, z)
+        load_prior(1, 0)
+        load_prior(1, 1)
         nc.sync.dma_start(
             out=b_words[:].rearrange("p g n -> p (g n)").bitcast(I32).rearrange("p (g n) -> p g n", g=2),
             in_=basis_words.bitcast(I32).rearrange("g p n -> p g n"),
@@ -127,6 +128,11 @@ def tile_hrtf_weights_synthesis_s8_kernel(
 
         x_banks = {}
 
+        def warm(n, rhs):
+            b = bank()
+            for k in range(n):
+                nc.tensor.matmul(b[:], lhsT=zeros[:, 0:P], rhs=rhs, start=True, stop=True)
+
         def x_turn(i):
             for q in range(3):
                 b = bank()
@@ -139,11 +145,8 @@ def tile_hrtf_weights_synthesis_s8_kernel(
                         nc.tensor.transpose(
                             x_banks[i, q][:, col:col + P], xw[:, 256 * q + u:256 * (q + 1):2], ident[:]
                         )
-
-        def warm(n):
-            b = bank()
-            for k in range(n):
-                nc.tensor.matmul(b[:], lhsT=zeros[:, 0:P], rhs=zeros[:], start=True, stop=True)
+                if i < 3:
+                    warm(1, zeros[:])
 
         def copy(engine, out, in_):
             if engine == "S":
@@ -163,13 +166,12 @@ def tile_hrtf_weights_synthesis_s8_kernel(
                 x_banks[i, q][:].rearrange("p (a u m) -> p a m u", a=2, u=2),
             )
 
-        def x_quant(i):
-            for q0, q1 in ((0, 2), (2, 3)):
-                nc.vector.quantize_mx(
-                    out=x_c[i][:, q0:q1, :].rearrange("p q m -> p (q m)").bitcast(E4M3),
-                    scales=x_s[i][:, q0:q1, :].rearrange("p q m -> p (q m)"),
-                    in_=x_grouped[i][:, q0:q1].rearrange("p q a m t -> p (q a m t)"),
-                )
+        def x_quant(i, q0, q1):
+            nc.vector.quantize_mx(
+                out=x_c[i][:, q0:q1, :].rearrange("p q m -> p (q m)").bitcast(E4M3),
+                scales=x_s[i][:, q0:q1, :].rearrange("p q m -> p (q m)"),
+                in_=x_grouped[i][:, q0:q1].rearrange("p q a m t -> p (q a m t)"),
+            )
 
         w_grouped = {}
 
@@ -268,8 +270,8 @@ def tile_hrtf_weights_synthesis_s8_kernel(
                 out=mag_tiles[i][:, 512 * f:512 * (f + 1)], in_=mag_banks[i, f][:], func=EXP, scale=depth_f[:, i:i + 1]
             )
 
-        def mag_store(i, z):
-            cols = slice(1024 * z, 1024 * (z + 1))
+        def mag_store(i, c0, c1):
+            cols = slice(c0, c1)
             nc.sync.dma_start(out=mag_rows[i // 4, i % 4, :, cols], in_=mag_tiles[i][:, cols])
 
         h_grouped = {}
@@ -360,76 +362,91 @@ def tile_hrtf_weights_synthesis_s8_kernel(
             for q in range(3):
                 x_empty(i, q, "V" if q in vector_banks else "S")
 
+        def x_quants(i):
+            x_quant(i, 0, 2)
+            x_quant(i, 2, 3)
+
         def w_step(h, q):
             w_group(h, q, "V")
             w_group(h, q, "S")
 
-        def h_all(i, h):
-            for q in range(3):
-                h_pass(i, h, q)
+        def h_passes(tiles, h, passes):
+            for q in passes:
+                for i in tiles:
+                    h_pass(i, h, q)
 
-        def mag_step(i):
+        def h_all(i, h):
+            h_passes((i,), h, range(3))
+
+        def mag_step(i, run=2):
             for f in range(4):
                 mag_mm(i, f)
                 mag_exp(i, f)
-                if f % 2:
-                    mag_store(i, f // 2)
+                if (f + 1) % run == 0:
+                    mag_store(i, 512 * (f + 1 - run), 512 * (f + 1))
 
-        def load_step(a, engines, halves=1):
+        def load_step(a, engines):
             for h in range(2):
                 load_mm(a, h)
                 load_empty(a, h, engines[h])
-            load_store(a, halves)
+            load_store(a, 1)
 
-        warm(8)
-        w_step(0, 0)
+        warm(8, zeros[:])
         x_turn(0)
+        w_step(0, 0)
+        w_step(0, 1)
         x_step(0, (1,))
         w_quant(0, 0)
-        w_step(0, 1)
-        x_quant(0)
-        warm(2)
-        x_turn(1)
-        x_step(1, (1,))
+        x_quants(0)
         w_quant(0, 1)
-        x_quant(1)
+        warm(2, w_raw[0][0][:, 0, :])
+        warm(2, w_raw[0][1][:, 0, :])
+        x_turn(1)
+        x_step(1, (0,))
         x_turn(2)
-        w_step(0, 2)
-        x_step(2, (0, 1))
+        x_quant(1, 0, 2)
+        w_group(0, 2, "V")
+        x_step(2, (2,))
+        w_group(0, 2, "S")
+        x_quants(2)
+        x_quant(1, 2, 3)
         w_quant(0, 2)
-        x_quant(2)
-        for q in range(2):
-            for i in range(4):
-                h_pass(i, 0, q)
+        h_passes(range(4), 0, (0,))
         x_turn(3)
+        x_step(3, ())
+        h_passes(range(4), 0, (1, 2))
         w_step(1, 0)
-        x_step(3, (1,))
-        w_quant(1, 0)
-        x_quant(3)
-        for i in range(4):
-            h_pass(i, 0, 2)
+        x_quant(3, 0, 2)
+        w_step(1, 1)
+        x_quant(3, 2, 3)
         h_all(4, 0)
         h_all(5, 0)
-        w_step(1, 1)
-        w_step(1, 2)
-        w_quant(1, 1)
         h_add(0, 0)
+        w_quant(1, 0)
+        h_add(1, 0)
+        w_quant(1, 1)
+        h_add(2, 0)
+        w_step(1, 2)
+        h_add(3, 0)
         w_quant(1, 2)
-        for i in range(1, 6):
-            if i == 4:
-                h_all(0, 1)
-                h_all(1, 1)
-            h_add(i, 0)
-        h_all(2, 1)
+        h_all(6, 0)
+        h_add(4, 0)
+        h_add(5, 0)
+        h_passes((0, 1), 1, (0, 1))
+        h_all(7, 0)
+        h_passes((2,), 1, (0, 1))
+        h_passes((0, 1, 2), 1, (2,))
         h_all(3, 1)
         for i in range(4):
             h_add(i, 1)
-        h_all(6, 0)
-        h_all(7, 0)
+        h_all(4, 1)
+        h_all(5, 1)
+        h_add(4, 1)
+        h_add(5, 1)
         for i in range(4):
             ht_turn(i)
         for i in range(4):
-            ht_empty(i, "SSSV"[i])
+            ht_empty(i, "SSVS"[i])
         h_add(6, 0)
         ht_quant(0)
         ht_quant(1)
@@ -437,49 +454,49 @@ def tile_hrtf_weights_synthesis_s8_kernel(
         ht_quant(2)
         ht_quant(3)
         nc.vector.tensor_copy(out=depth_f[:], in_=depth_bf[:].rearrange("p g t -> p (g t)"))
+        h_all(6, 1)
+        h_all(7, 1)
+        pop_product(0)
         h_group(0, 0, "S")
-        for i in range(4, 8):
-            h_all(i, 1)
-        for i in range(4, 8):
-            h_add(i, 1)
         mag_step(0)
+        h_add(6, 1)
+        h_add(7, 1)
         mag_step(1)
         h_group(0, 1, "V")
-        pop_product(0)
+        h_quant(0, 0)
+        pop_product(1)
         h_quant(0, 1)
         for i in range(4, 8):
             ht_turn(i)
-        ht_empty(4, "V")
-        ht_empty(5, "S")
-        pop_product(1)
-        ht_empty(6, "V")
-        ht_empty(7, "S")
+        ht_empty(4, "S")
+        ht_empty(5, "V")
+        pop_product(2)
+        ht_empty(6, "S")
+        ht_empty(7, "V")
         ht_quant(4)
         ht_quant(5)
-        pop_product(2)
         mag_step(2)
         pop_product(3)
         ht_quant(6)
         ht_quant(7)
+        h_group(1, 0, "V")
         mag_step(3)
-        h_quant(0, 0)
-        mag_step(4)
         for z in range(2):
             for g in range(2):
                 pop_turn(g, z)
         for z in range(2):
             for g in range(2):
-                pop_empty(g, z, "VS"[z])
-        h_group(1, 0, "V")
-        pop_quant(0)
-        pop_quant(1)
+                pop_empty(g, z, "VS"[g])
+        mag_step(4)
         h_quant(1, 0)
+        pop_quant(0)
         h_group(1, 1, "V")
+        pop_quant(1)
         h_quant(1, 1)
         mag_step(5)
         mag_step(6)
         load_step(0, "VV")
-        load_step(1, "VS")
-        load_step(2, "VV")
-        mag_step(7)
-        load_step(3, "VS", halves=2)
+        load_step(1, "VV")
+        load_step(2, "VS")
+        load_step(3, "VS")
+        mag_step(7, run=1)

from contextlib import ExitStack

import concourse.mybir as mybir
from concourse.masks import make_identity

M, K, C, F, R = 1024, 1536, 1024, 2048, 512
FLOPS = 2 * (M * K * C + M * C * F + R * M * C)

F32 = mybir.dt.float32
BF16 = mybir.dt.bfloat16
U32 = mybir.dt.uint32
I32 = mybir.dt.int32
U8 = mybir.dt.uint8
E4M3 = mybir.dt.float8_e4m3fn_x4
E2M1 = mybir.dt.float4_e2m1fn_x4
FP8 = mybir.dt.float8_e4m3fn
ADD = mybir.AluOpType.add
MULT = mybir.AluOpType.mult
EXP = mybir.ActivationFunctionType.Exp

P = 128
HALF = 512
V_COLS = (256, 224)


def tile_hrtf_weights_synthesis_s8_kernel(
    tc, x, w, prior, basis_words, basis_scales, depth, pop_bytes, pop_scale, mag, load
):
    nc = tc.nc
    with ExitStack() as ctx:
        keep = ctx.enter_context(tc.tile_pool(name="keep", bufs=1))
        stage = ctx.enter_context(tc.tile_pool(name="stage", bufs=4))
        outs = ctx.enter_context(tc.tile_pool(name="outs", bufs=3))
        psum = ctx.enter_context(tc.psum_pool(name="psum", bufs=8))
        ctx.enter_context(tc.manual_schedule())

        def bank():
            b = psum.tile([P, 512], F32, name="bank")
            return b

        def kept(name, shape, dt):
            t = keep.tile(shape, dt, name=name, align_bytes=64)
            return t

        ident = kept("ident", [P, P], F32)
        dummy = kept("dummy", [P, 1], F32)
        zeros = kept("zeros", [P, 512], BF16)
        x_raw = [
            outs.tile([P, 2, K], BF16, name="x_raw%d" % i, tag="big", bufs=4, align_bytes=64) for i in range(4)
        ]
        w_raw = [
            [
                outs.tile([P, 4, HALF], BF16, name="w_raw%d%d" % (h, q), tag="small", bufs=6, align_bytes=64)
                for q in range(3)
            ]
            for h in range(2)
        ]
        pr = [[kept("pr%d%d" % (g, z), [P, 2, C], BF16) for z in range(2)] for g in range(2)]
        b_words = kept("b_words", [P, 2, 2 * F], U8)
        b_scales = kept("b_scales", [P, 2, F], U8)
        depth_bf = kept("depth_bf", [P, 2, 4], BF16)
        depth_f = kept("depth_f", [P, 8], F32)
        pop_raw = kept("pop_raw", [P, 4, M], U8)
        pop_sc = kept("pop_sc", [P, M], F32)
        pop_bf = kept("pop_bf", [P, 4, M], BF16)
        x_c = [kept("x_c%d" % i, [P, 3, 256], U32) for i in range(4)]
        x_s = [kept("x_s%d" % i, [P, 3, 256], U8) for i in range(4)]
        w_c = [[kept("w_c%d%d" % (h, q), [P, HALF], U32) for q in range(3)] for h in range(2)]
        w_s = [[kept("w_s%d%d" % (h, q), [P, HALF], U8) for q in range(3)] for h in range(2)]
        hb = [kept("hb%d" % g, [P, 4, C], BF16) for g in range(2)]
        ht_c = [kept("ht_c%d" % i, [P, 2, P], U32) for i in range(8)]
        ht_s = [kept("ht_s%d" % i, [P, 2, P], U8) for i in range(8)]
        h_c = [kept("h_c%d" % g, [P, C], U32) for g in range(2)]
        h_s = [kept("h_s%d" % g, [P, C], U8) for g in range(2)]
        p_c = [kept("p_c%d" % g, [P, R], U32) for g in range(2)]
        p_s = [kept("p_s%d" % g, [P, R], U8) for g in range(2)]

        nc.vector.memset(zeros[:], 0.0)
        nc.vector.memset(dummy[:], 0.0)
        nc.scalar.activation(out=dummy[:], in_=dummy[:], func=EXP)
        make_identity(nc, ident[:])
        nc.gpsimd.memset(b_scales[:].rearrange("p g n -> p (g n)").bitcast(I32), 0)

        def load_x(i):
            g, t0 = i // 2, 2 * (i % 2)
            src = x[g * 512:(g + 1) * 512, :].rearrange("(p t) k -> p t k", t=4)
            for a in range(2):
                nc.sync.dma_start(out=x_raw[i][:, a, :], in_=src[:, t0 + a, :])

        def load_w(h, q):
            src = w[q * 512:(q + 1) * 512, h * HALF:(h + 1) * HALF]
            nc.sync.dma_start(out=w_raw[h][q][:], in_=src.rearrange("(p j) c -> p j c", j=4))

        def load_prior(g, z):
            src = prior[g * 512:(g + 1) * 512, :].rearrange("(p t) c -> p t c", t=4)
            nc.sync.dma_start(out=pr[g][z][:], in_=src[:, 2 * z:2 * z + 2, :])

        load_x(0)
        load_w(0, 0)
        load_w(0, 1)
        load_x(1)
        load_x(2)
        load_w(0, 2)
        load_x(3)
        load_w(1, 0)
        load_w(1, 1)
        load_prior(0, 0)
        load_prior(0, 1)
        load_w(1, 2)
        load_prior(1, 0)
        load_prior(1, 1)
        nc.sync.dma_start(
            out=b_words[:].rearrange("p g n -> p (g n)").bitcast(I32).rearrange("p (g n) -> p g n", g=2),
            in_=basis_words.bitcast(I32).rearrange("g p n -> p g n"),
        )
        b_scales_i = b_scales[:].rearrange("p g n -> p (g n)").bitcast(I32).rearrange("p (g n) -> p g n", g=2)
        for quad in range(4):
            nc.sync.dma_start(
                out=b_scales_i[32 * quad:32 * quad + 4],
                in_=basis_scales.bitcast(I32)[:, 4 * quad:4 * quad + 4, :].rearrange("g r n -> r g n"),
            )
        nc.sync.dma_start(out=depth_bf[:], in_=depth.rearrange("(g p t) -> p g t", p=P, t=4))
        nc.sync.dma_start(out=pop_raw[:], in_=pop_bytes.rearrange("(p a) k -> p a k", a=4))
        nc.sync.dma_start(out=pop_sc[:], in_=pop_scale.rearrange("o k -> (o k)").partition_broadcast(P))

        def words(tile_ap):
            return tile_ap.bitcast(F32)

        x_banks = {}

        def warm(n, rhs):
            b = bank()
            for k in range(n):
                nc.tensor.matmul(b[:], lhsT=zeros[:, 0:P], rhs=rhs, start=True, stop=True)

        def x_turn(i):
            for q in range(3):
                b = bank()
                x_banks[i, q] = b
            for a in range(2):
                xw = words(x_raw[i][:, a, :])
                for q in range(3):
                    for u in range(2):
                        col = (2 * a + u) * P
                        nc.tensor.transpose(
                            x_banks[i, q][:, col:col + P], xw[:, 256 * q + u:256 * (q + 1):2], ident[:]
                        )
                if i < 3:
                    warm(1, zeros[:])

        def copy(engine, out, in_):
            if engine == "S":
                nc.scalar.copy(out=out, in_=in_)
            else:
                nc.vector.tensor_copy(out=out, in_=in_)

        x_grouped = {}

        def x_empty(i, q, engine):
            if i not in x_grouped:
                xg = stage.tile([P, 3, 2, P, 4], BF16, name="xg", bufs=2, align_bytes=64)
                x_grouped[i] = xg
            copy(
                engine,
                words(x_grouped[i][:, q].rearrange("p a m t -> p (a m t)")).rearrange("p (a m u) -> p a m u", a=2, u=2),
                x_banks[i, q][:].rearrange("p (a u m) -> p a m u", a=2, u=2),
            )

        def x_quant(i, q0, q1):
            nc.vector.quantize_mx(
                out=x_c[i][:, q0:q1, :].rearrange("p q m -> p (q m)").bitcast(E4M3),
                scales=x_s[i][:, q0:q1, :].rearrange("p q m -> p (q m)"),
                in_=x_grouped[i][:, q0:q1].rearrange("p q a m t -> p (q a m t)"),
            )

        w_grouped = {}

        def w_group(h, q, engine):
            if (h, q) not in w_grouped:
                wg = stage.tile([P, HALF, 4], BF16, name="wg", bufs=3, align_bytes=64)
                w_grouped[h, q] = wg
            cols = slice(0, V_COLS[h]) if engine == "V" else slice(V_COLS[h], HALF)
            copy(engine, w_grouped[h, q][:, cols, :], w_raw[h][q][:, :, cols].rearrange("p j c -> p c j"))

        def w_quant(h, q):
            nc.vector.quantize_mx(
                out=w_c[h][q][:].bitcast(E4M3),
                scales=w_s[h][q][:],
                in_=w_grouped[h, q][:].rearrange("p c j -> p (c j)"),
            )

        h_banks = {}

        def h_pass(i, h, q):
            if q == 0:
                b = bank()
                h_banks[i, h] = b
            cols = slice((i % 2) * P, (i % 2 + 1) * P)
            nc.tensor.matmul_mx(
                out=h_banks[i, h][:],
                lhsT=x_c[i // 2][:, q, cols].bitcast(E4M3),
                lhsT_scale=x_s[i // 2][:, q, cols],
                rhs=w_c[h][q][:].bitcast(E4M3),
                rhs_scale=w_s[h][q][:],
                start=(q == 0),
                stop=(q == 2),
            )

        def h_add(i, h):
            g, t = i // 4, i % 4
            nc.vector.tensor_tensor(
                out=hb[g][:, t, h * HALF:(h + 1) * HALF].rearrange("q (u p e) -> q u p e", u=2, e=2),
                in0=h_banks[i, h][:].rearrange("q (p u e) -> q u p e", u=2, e=2),
                in1=pr[g][t // 2][:, t % 2, h * HALF:(h + 1) * HALF].rearrange("q (p u e) -> q u p e", u=2, e=2),
                op=ADD,
            )

        ht_banks = {}

        def ht_turn(i):
            g, t = i // 4, i % 4
            b = bank()
            ht_banks[i] = b
            hw = words(hb[g][:, t, :])
            for v in range(4):
                nc.tensor.transpose(b[:, v * P:(v + 1) * P], hw[:, v * P:(v + 1) * P], ident[:])

        ht_grouped = {}

        def ht_empty(i, engine):
            hg = stage.tile([P, 2, P, 4], BF16, name="hg", align_bytes=64)
            ht_grouped[i] = hg
            copy(
                engine,
                words(hg[:].rearrange("p a m t -> p (a m t)")).rearrange("p (a m u) -> p a m u", a=2, u=2),
                ht_banks[i][:].rearrange("p (a u m) -> p a m u", a=2, u=2),
            )

        def ht_quant(i):
            nc.vector.quantize_mx(
                out=ht_c[i][:].rearrange("p a m -> p (a m)").bitcast(E4M3),
                scales=ht_s[i][:].rearrange("p a m -> p (a m)"),
                in_=ht_grouped[i][:].rearrange("p a m t -> p (a m t)"),
            )

        mag_rows = mag.rearrange("(g p t) f -> g t p f", p=P, t=4)
        mag_banks = {}

        def mag_mm(i, f):
            b = bank()
            mag_banks[i, f] = b
            for a in range(2):
                nc.tensor.matmul_mx(
                    out=b[:],
                    lhsT=ht_c[i][:, a, :].bitcast(E4M3),
                    lhsT_scale=ht_s[i][:, a, :],
                    rhs=b_words[:, a, 1024 * f:1024 * (f + 1)].bitcast(E2M1),
                    rhs_scale=b_scales[:, a, 512 * f:512 * (f + 1)],
                    start=(a == 0),
                    stop=(a == 1),
                )

        mag_tiles = {}

        def mag_exp(i, f):
            if f == 0:
                mo = outs.tile([P, F], F32, name="mo", tag="big", bufs=4, align_bytes=64)
                mag_tiles[i] = mo
            nc.scalar.activation(
                out=mag_tiles[i][:, 512 * f:512 * (f + 1)], in_=mag_banks[i, f][:], func=EXP, scale=depth_f[:, i:i + 1]
            )

        def mag_store(i, c0, c1):
            cols = slice(c0, c1)
            nc.sync.dma_start(out=mag_rows[i // 4, i % 4, :, cols], in_=mag_tiles[i][:, cols])

        h_grouped = {}

        def h_group(g, h, engine):
            group = stage.tile([P, HALF, 4], BF16, name="group", bufs=3, align_bytes=64)
            h_grouped[g, h] = group
            cols = slice(HALF * h, HALF * (h + 1))
            copy(engine, group[:], hb[g][:, :, cols].rearrange("p t c -> p c t"))

        def h_quant(g, h):
            cols = slice(HALF * h, HALF * (h + 1))
            nc.vector.quantize_mx(
                out=h_c[g][:, cols].bitcast(E4M3),
                scales=h_s[g][:, cols],
                in_=h_grouped[g, h][:].rearrange("p c t -> p (c t)"),
            )

        pop_banks = {}

        def pop_product(a):
            nc.vector.tensor_tensor(out=pop_bf[:, a, :], in0=pop_raw[:, a, :].bitcast(FP8), in1=pop_sc[:], op=MULT)

        def pop_turn(g, z):
            b = bank()
            pop_banks[g, z] = b
            for a in range(2):
                pw = words(pop_bf[:, 2 * z + a, :])
                for u in range(2):
                    col = (2 * a + u) * P
                    nc.tensor.transpose(b[:, col:col + P], pw[:, 256 * g + u:256 * (g + 1):2], ident[:])

        pop_grouped = {}

        def pop_empty(g, z, engine):
            if g not in pop_grouped:
                group = stage.tile([P, 2, 2, P, 4], BF16, name="group", bufs=3, align_bytes=64)
                pop_grouped[g] = group
            copy(
                engine,
                words(pop_grouped[g][:, z].rearrange("p a r t -> p (a r t)")).rearrange("p (a r u) -> p a r u", a=2, u=2),
                pop_banks[g, z][:].rearrange("p (a u r) -> p a r u", a=2, u=2),
            )

        def pop_quant(g):
            nc.vector.quantize_mx(
                out=p_c[g][:].bitcast(E4M3),
                scales=p_s[g][:],
                in_=pop_grouped[g][:].rearrange("p z a r t -> p (z a r t)"),
            )

        load_rows = load.rearrange("(p a) c -> a p c", a=4)
        load_banks = {}

        def load_mm(a, h):
            b = bank()
            load_banks[a, h] = b
            for g in range(2):
                nc.tensor.matmul_mx(
                    out=b[:],
                    lhsT=p_c[g][:, P * a:P * (a + 1)].bitcast(E4M3),
                    lhsT_scale=p_s[g][:, P * a:P * (a + 1)],
                    rhs=h_c[g][:, 512 * h:512 * (h + 1)].bitcast(E4M3),
                    rhs_scale=h_s[g][:, 512 * h:512 * (h + 1)],
                    start=(g == 0),
                    stop=(g == 1),
                )

        load_tiles = {}

        def load_empty(a, h, engine):
            if a not in load_tiles:
                lo = outs.tile([P, C], F32, name="lo", tag="small", bufs=6, align_bytes=64)
                load_tiles[a] = lo
            copy(
                engine,
                load_tiles[a][:, 512 * h:512 * (h + 1)].rearrange("q (p u e) -> q p u e", u=2, e=2),
                load_banks[a, h][:].rearrange("q (u p e) -> q p u e", u=2, e=2),
            )

        def load_store(a, halves):
            for h in range(halves):
                cols = slice(C // halves * h, C // halves * (h + 1))
                nc.sync.dma_start(out=load_rows[a, :, cols], in_=load_tiles[a][:, cols])


        def x_step(i, vector_banks):
            for q in range(3):
                x_empty(i, q, "V" if q in vector_banks else "S")

        def x_quants(i):
            x_quant(i, 0, 2)
            x_quant(i, 2, 3)

        def w_step(h, q):
            w_group(h, q, "V")
            w_group(h, q, "S")

        def h_passes(tiles, h, passes):
            for q in passes:
                for i in tiles:
                    h_pass(i, h, q)

        def h_all(i, h):
            h_passes((i,), h, range(3))

        def mag_step(i, run=2):
            for f in range(4):
                mag_mm(i, f)
                mag_exp(i, f)
                if (f + 1) % run == 0:
                    mag_store(i, 512 * (f + 1 - run), 512 * (f + 1))

        def load_step(a, engines):
            for h in range(2):
                load_mm(a, h)
                load_empty(a, h, engines[h])
            load_store(a, 1)

        warm(8, zeros[:])
        x_turn(0)
        w_step(0, 0)
        w_step(0, 1)
        x_step(0, (1,))
        w_quant(0, 0)
        x_quants(0)
        w_quant(0, 1)
        warm(2, w_raw[0][0][:, 0, :])
        warm(2, w_raw[0][1][:, 0, :])
        x_turn(1)
        x_step(1, (0,))
        x_turn(2)
        x_quant(1, 0, 2)
        w_group(0, 2, "V")
        x_step(2, (2,))
        w_group(0, 2, "S")
        x_quants(2)
        x_quant(1, 2, 3)
        w_quant(0, 2)
        h_passes(range(4), 0, (0,))
        x_turn(3)
        x_step(3, ())
        h_passes(range(4), 0, (1, 2))
        w_step(1, 0)
        x_quant(3, 0, 2)
        w_step(1, 1)
        x_quant(3, 2, 3)
        h_all(4, 0)
        h_all(5, 0)
        h_add(0, 0)
        w_quant(1, 0)
        h_add(1, 0)
        w_quant(1, 1)
        h_add(2, 0)
        w_step(1, 2)
        h_add(3, 0)
        w_quant(1, 2)
        h_all(6, 0)
        h_add(4, 0)
        h_add(5, 0)
        h_passes((0, 1), 1, (0, 1))
        h_all(7, 0)
        h_passes((2,), 1, (0, 1))
        h_passes((0, 1, 2), 1, (2,))
        h_all(3, 1)
        for i in range(4):
            h_add(i, 1)
        h_all(4, 1)
        h_all(5, 1)
        h_add(4, 1)
        h_add(5, 1)
        for i in range(4):
            ht_turn(i)
        for i in range(4):
            ht_empty(i, "SSVS"[i])
        h_add(6, 0)
        ht_quant(0)
        ht_quant(1)
        h_add(7, 0)
        ht_quant(2)
        ht_quant(3)
        nc.vector.tensor_copy(out=depth_f[:], in_=depth_bf[:].rearrange("p g t -> p (g t)"))
        h_all(6, 1)
        h_all(7, 1)
        pop_product(0)
        h_group(0, 0, "S")
        mag_step(0)
        h_add(6, 1)
        h_add(7, 1)
        mag_step(1)
        h_group(0, 1, "V")
        h_quant(0, 0)
        pop_product(1)
        h_quant(0, 1)
        for i in range(4, 8):
            ht_turn(i)
        ht_empty(4, "S")
        ht_empty(5, "V")
        pop_product(2)
        ht_empty(6, "S")
        ht_empty(7, "V")
        ht_quant(4)
        ht_quant(5)
        mag_step(2)
        pop_product(3)
        ht_quant(6)
        ht_quant(7)
        h_group(1, 0, "V")
        mag_step(3)
        for z in range(2):
            for g in range(2):
                pop_turn(g, z)
        for z in range(2):
            for g in range(2):
                pop_empty(g, z, "VS"[g])
        mag_step(4)
        h_quant(1, 0)
        pop_quant(0)
        h_group(1, 1, "V")
        pop_quant(1)
        h_quant(1, 1)
        mag_step(5)
        mag_step(6)
        load_step(0, "VV")
        load_step(1, "VV")
        load_step(2, "VS")
        load_step(3, "VS")
        mag_step(7, run=1)
